import numpy as np
import ml_dtypes


def mxq(x, axis, fmt="e4m3"):
    dtype, down = {"e4m3": (ml_dtypes.float8_e4m3fn, 7), "e5m2": (ml_dtypes.float8_e5m2, 14)}[fmt]
    v = np.moveaxis(np.asarray(x, np.float32).astype(ml_dtypes.bfloat16).astype(np.float64), axis, -1)
    blocks = v.reshape(v.shape[:-1] + (-1, 32))
    amax = np.abs(blocks).max(-1, keepdims=True)
    byte = np.maximum(np.where(amax > 0, np.frexp(amax)[1] - 1 + 127, 0) - down, 1)
    scale = np.exp2(byte - 127.0)
    codes = (blocks / scale).astype(np.float32).astype(dtype).astype(np.float64)
    return np.moveaxis((codes * scale).reshape(v.shape), -1, axis)


WIDE = False


def mx_kscale(k):
    if not WIDE:
        return np.ones(k)
    levels = np.array([10, -10, 5, -5, 0])
    if k % 512:
        return np.exp2(np.random.permutation(np.resize(levels, k // 32))).repeat(32)
    a = np.empty((k // 512, 16))
    for p in range(k // 512):
        a[p, :8] = np.random.permutation(np.resize(levels, 8))
        for g in range(8):
            far = levels[np.abs(levels - a[p, g]) >= 10]
            a[p, g + 8] = far[np.random.randint(len(far))]
    return np.exp2(a.ravel()).repeat(32)


def f64(x):
    return np.asarray(x).astype(np.float64)


def striped8(idx):
    return np.concatenate([v.reshape(-1, 16).T for v in idx]).astype(np.uint16)


def unstriped8(offs):
    return np.stack([offs[16 * g:16 * g + 16].T.reshape(-1) for g in range(8)]).astype(np.int64)


E2M1 = np.array([0.0, 0.5, 1.0, 1.5, 2.0, 3.0, 4.0, 6.0, -0.0, -0.5, -1.0, -1.5, -2.0, -3.0, -4.0, -6.0])


def pack_weight(w, fmt):
    k, n = w.shape
    w = f64(np.asarray(w, np.float32).astype(ml_dtypes.bfloat16)).reshape(k // 32, 32, n)
    amax = np.abs(w).max(1)
    if fmt == "e4m3":
        byte = np.frexp(amax)[1] - 1 + 127 - 7
    else:
        mant, ex = np.frexp(amax / 6.0)
        byte = np.where(mant > 0.5, ex, ex - 1) + 127
    byte = np.clip(np.where(amax > 0, byte, 1), 1, 254)
    scaled = (w * np.exp2(127.0 - byte)[:, None, :]).reshape(k, n).astype(np.float32)
    by_word = np.ascontiguousarray(scaled.reshape(k // 512, 128, 4, n).transpose(0, 1, 3, 2))
    if fmt == "e4m3":
        words = by_word.astype(ml_dtypes.float8_e4m3fn).view(np.uint8)
    else:
        c = by_word.astype(ml_dtypes.float4_e2m1fn).view(np.uint8) & 0xF
        words = (c[..., 0::2] | (c[..., 1::2] << 4)).reshape(k // 512, 128, 2 * n)
    return np.ascontiguousarray(words), np.ascontiguousarray(byte.astype(np.uint8).reshape(k // 512, 16, n))


def unpack_weight(words, scales, fmt):
    g, _, n = scales.shape
    words = np.ascontiguousarray(words).reshape(g, 128, n, -1)
    if fmt == "e4m3":
        vals = words.view(ml_dtypes.float8_e4m3fn).astype(np.float64)
    else:
        nib = np.empty((g, 128, n, 4), np.uint8)
        nib[..., 0::2] = words & 0xF
        nib[..., 1::2] = words >> 4
        vals = E2M1[nib]
    vals = vals * np.repeat(np.exp2(scales.astype(np.float64) - 127.0), 8, axis=1)[..., None]
    return vals.transpose(0, 1, 3, 2).reshape(g * 512, n)


K, M, T, S = 512, 1024, 1024, 512


def setup_inputs():
    n = np.random.standard_normal
    s = mx_kscale(K)[:, None]
    p_w = pack_weight(n((K, M)) / np.sqrt(K) / s, "e4m3")
    return {
        "xT": (n((K, T)) * s).astype(np.float32),
        "w_words": p_w[0],
        "w_scales": p_w[1],
        "wgt": np.repeat(np.random.uniform(0.5, 2.0, (8, S)), 16, axis=0).astype(np.float32),
        "b": (0.3 * n(1024)).astype(np.float32),
        "wgo": np.repeat(np.random.uniform(0.5, 2.0, (8, S)), 16, axis=0).astype(np.float32),
        "offs": striped8(np.stack([np.random.permutation(T)[:S] for _ in range(8)])),
        "offs2": striped8(np.stack([np.random.permutation(T)[:S] for _ in range(8)])),
    }


def reference(xT, w_words, w_scales, wgt, b, wgo, offs, offs2):
    idx = unstriped8(offs)
    group = np.arange(K) % 512 // 64
    xg = f64(wgt)[np.arange(K) // 4 % 128] * f64(xT)[np.arange(K)[:, None], idx[group]]
    xT_ = mxq(xg, 0, "e4m3")
    w_ = unpack_weight(w_words, w_scales, "e4m3")
    y = w_.T @ xT_
    place = unstriped8(offs2)[np.arange(M) % 128 // 16]
    out = np.zeros((M, T))
    out[np.arange(M)[:, None], place] = f64(wgo)[np.arange(M) % 128] * (y + f64(b)[:, None])
    return out

import concourse.mybir as mybir
from concourse.masks import make_identity

K, M, T, S = 512, 1024, 1024, 512
FLOPS = 2 * K * M * S

F32 = mybir.dt.float32
BF16 = mybir.dt.bfloat16
I32 = mybir.dt.int32
U32 = mybir.dt.uint32
U16 = mybir.dt.uint16
U8 = mybir.dt.uint8
FP8X4 = mybir.dt.float8_e4m3fn_x4
MULT = mybir.AluOpType.mult
IDENTITY = mybir.ActivationFunctionType.Identity

P = 128
PLANES = 4
HALF = S // 2
N_TILES = M // P


def tile_list_hboth_bias_kernel(tc, xT, w_words, w_scales, wgt, b, wgo, offs, offs2, out):
    nc = tc.nc
    with (
        tc.tile_pool(name="keep", bufs=1) as keep,
        tc.tile_pool(name="sums", bufs=16) as sums,
        tc.psum_pool(name="psum", bufs=8) as psum,
    ):
        offs_in = keep.tile([P, S // 16], U16, name="offs_in")
        offs_out = keep.tile([P, S // 16], U16, name="offs_out")
        wgt_sb = [keep.tile([P, HALF], F32, name=f"wgt{h}") for h in range(2)]
        wgo_sb = keep.tile([P, S], F32, name="wgo_sb")
        planes = [keep.tile([P, T], F32, name=f"plane{i}") for i in range(PLANES)]
        w_sb = keep.tile([P, M], U32, name="w_sb", align_bytes=256)
        ws_sb = keep.tile([P, M], U8, name="ws_sb", align_bytes=256)
        b_rows = keep.tile([P, P], F32, name="b_rows")
        ident = keep.tile([P, P], F32, name="ident")
        b_cols = keep.tile([P, N_TILES], F32, name="b_cols")
        warm = keep.tile([P, 1], F32, name="warm")
        windows = [keep.tile([P, T], F32, name=f"window{m}") for m in range(N_TILES)]
        picked = [keep.tile([P, PLANES, HALF], F32, name=f"picked{h}") for h in range(2)]
        grouped = [keep.tile([P, HALF, PLANES], BF16, name=f"grouped{h}", align_bytes=256) for h in range(2)]
        codes = [keep.tile([P, HALF], U32, name=f"codes{h}", align_bytes=256) for h in range(2)]
        scales = [keep.tile([P, HALF], U8, name=f"scales{h}", align_bytes=256) for h in range(2)]

        x_view = xT.rearrange("(p i) t -> p i t", i=PLANES)
        nc.sync.dma_start(offs_in[:], offs)
        nc.scalar.dma_start(out=wgt_sb[0][:], in_=wgt[:, 0:HALF])
        nc.sync.dma_start(out=planes[0][:], in_=x_view[:, 0, :])
        nc.scalar.dma_start(out=wgt_sb[1][:], in_=wgt[:, HALF:S])
        for i in range(1, PLANES):
            nc.sync.dma_start(out=planes[i][:], in_=x_view[:, i, :])

        nc.vector.memset(warm[:], 0.0)
        nc.scalar.activation(warm[:], warm[:], IDENTITY, bias=warm[:, 0:1])

        nc.gpsimd.memset(ws_sb[:].bitcast(I32), 0)
        nc.gpsimd.memset(b_rows[:], 0.0)
        make_identity(nc, ident[:])
        for q in range(4):
            nc.sync.dma_start(
                out=ws_sb[32 * q : 32 * q + 4, :].bitcast(I32), in_=w_scales[0, 4 * q : 4 * q + 4, :].bitcast(I32)
            )
        nc.sync.dma_start(out=b_rows[0:N_TILES, :], in_=b.rearrange("(m p) -> m p", p=P))
        for c in range(2):
            cols = slice(c * M // 2, (c + 1) * M // 2)
            nc.sync.dma_start(
                out=w_sb[:, cols].bitcast(I32), in_=w_words[0, :, cols, :].rearrange("p n t -> p (n t)").bitcast(I32)
            )
        nc.sync.dma_start(offs_out[:], offs2)
        nc.sync.dma_start(out=wgo_sb[:], in_=wgo)

        for m in range(5):
            nc.vector.memset(windows[m][:], 0.0)
        for m in range(5, N_TILES):
            nc.gpsimd.memset(windows[m][:], 0.0)

        b_psum = psum.tile([P, S], F32, name="b_psum", tag="acc")
        nc.tensor.transpose(b_psum[:, 0:P], b_rows[:], ident[:])
        nc.scalar.copy(out=b_cols[:], in_=b_psum[:, 0:N_TILES])

        half_cols = HALF // 16

        def gather(h, i):
            nc.vector.tensor_tensor(
                picked[h][:, i, :],
                planes[i][:].indirect(offs_in[:, h * half_cols : (h + 1) * half_cols]),
                wgt_sb[h][:],
                MULT,
            )

        def interleave(engine_copy, h):
            engine_copy(out=grouped[h][:], in_=picked[h][:].rearrange("p i w -> p w i"))

        def quantise(h):
            nc.vector.quantize_mx(
                out=codes[h][:].bitcast(FP8X4), scales=scales[h][:], in_=grouped[h][:].rearrange("p w i -> p (w i)")
            )

        accs = [None] * N_TILES
        results = {}

        def project(h, m):
            if h == 0:
                acc = psum.tile([P, S], F32, name=f"acc{m}", tag="acc")
                accs[m] = acc
            cols = slice(m * P, (m + 1) * P)
            part = accs[m][:, h * HALF : (h + 1) * HALF]
            nc.tensor.matmul_mx(
                out=part,
                lhsT=w_sb[:, cols].bitcast(FP8X4),
                lhsT_scale=ws_sb[:, cols],
                rhs=codes[h][:].bitcast(FP8X4),
                rhs_scale=scales[h][:],
                start=True,
                stop=True,
            )
            y = sums.tile([P, HALF], F32, name=f"y{h}_{m}", tag="y")
            nc.scalar.activation(y[:], part, IDENTITY, bias=b_cols[:, m : m + 1])
            results[(h, m)] = y

        def scatter(h, m):
            nc.vector.tensor_tensor(
                windows[m][:].indirect(offs_out[:, h * half_cols : (h + 1) * half_cols]),
                results[(h, m)][:],
                wgo_sb[:, h * HALF : (h + 1) * HALF],
                MULT,
            )

        gather(0, 0)
        gather(1, 0)
        gather(0, 1)
        gather(1, 1)
        gather(0, 2)
        gather(0, 3)
        interleave(nc.vector.tensor_copy, 0)
        gather(1, 2)
        quantise(0)
        gather(1, 3)
        for m in range(N_TILES):
            project(0, m)
            if m == 0:
                interleave(nc.scalar.copy, 1)
        scatter(0, 0)
        scatter(0, 1)
        quantise(1)
        for m in range(2, N_TILES):
            scatter(0, m)
        for m in range(N_TILES):
            project(1, m)
        for m in range(N_TILES):
            scatter(1, m)
            nc.sync.dma_start(out=out[m * P : (m + 1) * P, :], in_=windows[m][:])
